import numpy as np, ml_dtypes
CORES = [45,53,77,117,47,55,79,119]
N = 8
import mx_ref
NC, G = 128, 2
C = np.float32(0.043)
BF = ml_dtypes.bfloat16
def cut(t, i, w=512):
    return t[:, w * i:w * i + w]
def tile(rs):
    return np.stack(rs, axis=2).reshape(128, -1).astype(BF)
def layer(w, X):
    out = []
    for i in range(G):
        for t in range(len(X)):
            p = mx_ref.matmul(mx_ref.quantize(cut(w, len(X) * i + t)), X[t])
            z = p if t == 0 else z + p
        out.append(z)
    return out
def act(Z):
    return [np.maximum(s * z, 0) * C for z in Z for s in (1, -1)]
def pick(b):
    s = np.zeros((128, 128, 4), np.float32)
    s[np.arange(128), np.arange(128), b] = 1.0
    return mx_ref.quantize(s.reshape(128, 512).astype(BF))
def setup_inputs(rng):
    def f(*shape):
        return mx_ref.flush((rng.standard_normal(shape, dtype=np.float32) * np.exp2(rng.integers(-2, 3, shape[:-1] + (1,)))).astype(BF))
    return {"a": f(N, 128, G * 512), "b": f(N, 128, N * 4 * NC)}
def setup_inputs_blocks(rng):
    d = setup_inputs(rng)
    for k in ("a", "b"): d[k] = mx_ref.spread(d[k], rng, 4)
    return d
def setup_inputs_wide(rng):
    d = setup_inputs(rng)
    for k in ("a", "b"): d[k] = mx_ref.flush((d[k].astype(np.float32) * np.exp2(rng.integers(-8, 9, (N, 1, 1))).astype(np.float32)).astype(BF))
    return d
def reference(a, b):
    S = [pick(t) for t in range(4)]
    y = np.zeros((N, 128, NC, 4), np.float32)
    for c in range(N):
        for r in range(N):
            q = mx_ref.quantize(tile(act(layer(a[r], [mx_ref.quantize(cut(b[r], c, 4 * NC))]))))
            p = np.stack([mx_ref.matmul(S[t], q) for t in range(4)], axis=2)
            y[c] = p if r == 0 else y[c] + p
    return {"y": y.reshape(N, 128, 4 * NC)}

@@ -1,0 +1,315 @@
+from concourse.bass import DstId, RemoteDMATransfer
+from concourse.mybir import dt, AluOpType, ActivationFunctionType
+
+NR = 8
+W = 128
+E = 4 * W
+CF = 0.043
+
+SCRATCH = {
+    "a_t": ("sbuf", [128, 2 * E], "bfloat16"),
+    "b_t": ("sbuf", [128, NR * E], "bfloat16"),
+    "g_t": ("sbuf", [128, NR * E], "bfloat16"),
+    "S_t": ("sbuf", [128, 4 * E], "bfloat16"),
+    "a_q": ("sbuf", [128, 2 * W], "float8_e4m3fn_x4"),
+    "a_s": ("sbuf", [128, 2 * W], "uint8"),
+    "b_q": ("sbuf", [128, NR * W], "float8_e4m3fn_x4"),
+    "b_s": ("sbuf", [128, NR * W], "uint8"),
+    "g_q": ("sbuf", [128, NR * W], "float8_e4m3fn_x4"),
+    "g_s": ("sbuf", [128, NR * W], "uint8"),
+    "land_q": ("sbuf", [128, NR * W], "float8_e4m3fn_x4"),
+    "land_s": ("sbuf", [128, NR * W], "uint8"),
+    "S_q": ("sbuf", [128, 4 * W], "float8_e4m3fn_x4"),
+    "S_s": ("sbuf", [128, 4 * W], "uint8"),
+    "r_q": ("sbuf", [128, 2 * W], "float8_e4m3fn_x4"),
+    "r_s": ("sbuf", [128, 2 * W], "uint8"),
+    "y_t": ("sbuf", [128, E], "float32"),
+    "z": ("psum", [128, 4 * 512], "float32"),
+    "d": ("psum", [128, 4 * 512], "float32"),
+}
+SEMAPHORES = (["la", "qa", "s1", "s2", "s3", "s_in", "hq", "hs", "sent", "yc", "st"]
+              + ["%s%d" % (n, k) for n in ("lb", "qb", "ma", "mb", "r0", "as", "gq", "in") for k in range(NR)]
+              + ["dd%d" % b for b in range(4)])
+
+
+def _bits(m):
+    return [i for i in range(m.bit_length()) if (m >> i) & 1]
+
+
+def _mask(engines):
+    return sum(1 << i for i in engines)
+
+
+def _parts(engines, k):
+    n = len(engines) // k
+    return [engines[i * n:(i + 1) * n] for i in range(k)]
+
+
+def _plan(cores, topo):
+    n = len(cores)
+    every = range(topo.CHIPS * topo.CORES_PER_CHIP)
+    chips = []
+    for c in cores:
+        if topo.chip(c) not in chips:
+            chips.append(topo.chip(c))
+    members = {ch: [r for r in range(n) if topo.chip(cores[r]) == ch] for ch in chips}
+
+    def can(s, o):
+        return all(topo.may_write(s, cores[t]) for t in members[o])
+
+    ships = {r: [] for r in range(n)}
+    relays = {}
+    makes = {}
+    kind = {}
+    for ch in chips:
+        plane = [o for o in chips if o == ch or topo.same_plane(ch, o)]
+        near = [o for o in plane if o != ch]
+        far = [o for o in chips if o not in plane]
+        turn = plane.index(ch) % max(len(far), 1)
+        far = far[turn:] + far[:turn]
+        free = [k for k in every if topo.chip(k) == ch and k not in cores]
+        load = {}
+        own_way, handed, via = {}, {}, {}
+        for r in members[ch]:
+            s = cores[r]
+            open_ = [o for o in far + near if can(s, o)]
+            own_way[r] = open_[0]
+            handed[r] = [o for o in far + near if o != open_[0]]
+            load[topo.die(s)] = load.get(topo.die(s), 0) + 1
+        mine = []
+        for some in (far, near):
+            for r in members[ch]:
+                for o in handed[r]:
+                    if o in some:
+                        h = min([k for k in free if k not in mine and can(k, o)],
+                                key=lambda k: (load.get(topo.die(k), 0), k))
+                        mine.append(h)
+                        load[topo.die(h)] = load.get(topo.die(h), 0) + 1
+                        via[(r, o)] = h
+                        relays[h] = {"src": r, "dests": members[o], "jobs": []}
+        for r in members[ch]:
+            for i, o in enumerate(handed[r]):
+                ships[r].append((via[(r, o)], members[o]))
+                for t in members[o]:
+                    kind[(r, t)] = 3 + i
+            ships[r].append((None, members[own_way[r]]))
+            for t in members[own_way[r]]:
+                kind[(r, t)] = 2
+            for t in members[ch]:
+                if t != r:
+                    ships[r].append((None, [t]))
+                    kind[(r, t)] = 1
+            kind[(r, r)] = 0
+        for i, r in enumerate(members[ch]):
+            makes[r] = i
+        rest = [(b, r) for b in range(len(members[ch]), 4) for r in members[ch]]
+        for i, job in enumerate(rest):
+            relays[mine[i % len(mine)]]["jobs"].append(job)
+    return {"members": members, "ships": ships, "relays": relays, "makes": makes, "kind": kind}
+
+
+def _send(g, topo, items, local_sem):
+    if len(items) == 1:
+        dst, out, src, eng, rsem = items[0]
+        rid, pid, se = topo.addr(dst)
+        g.remote_dma(out, src, rsem, local_sem, pid, rid, _mask(eng))
+    else:
+        trs = []
+        for dst, out, src, eng, rsem in items:
+            rid, pid, se = topo.addr(dst)
+            trs.append(RemoteDMATransfer(dst_ids=[DstId(rid=rid, pnc=pid)], dma_engine_mask=_mask(eng),
+                                         remote_sem=rsem, src=src, dst=out))
+        g.remote_dma_fused(trs, local_sem=local_sem)
+    return sum(len(it[3]) for it in items)
+
+
+def _q(buf, lo, hi):
+    return buf[:, lo:hi].bitcast(dt.uint8)
+
+
+def _fan_engines(topo, src_core, cores, dests):
+    return _parts(_bits(topo.mask(src_core, cores[dests[0]])), len(dests))
+
+
+def _home_engines(topo, core, cores, plan, rank, dst):
+    on = _bits(topo.mask(core, cores[dst]))
+    away = [t for via, ds in plan["ships"][rank] if via is None for t in ds if topo.chip(cores[t]) != topo.chip(core)]
+    off = _bits(topo.mask(core, cores[away[0]])) if away else []
+    left = [e for e in on if e not in off]
+    return left if left else on
+
+
+def _make_S(g, T, b):
+    t = T.S_t[:, E * b:E * b + E]
+    g.vector.memset(t, 1.0).then_inc(T.sem.s1, 1)
+    g.wait_ge(T.sem.s1, 1)
+    g.affine_select(t, t, [[-1, E]], AluOpType.is_equal, 0.0, b, 4).then_inc(T.sem.s2, 1)
+    g.vector.wait_ge(T.sem.s2, 1)
+    g.vector.quantize_mx(T.S_q[:, W * b:W * b + W], T.S_s[:, W * b:W * b + W], t).then_inc(T.sem.s3, 1)
+    g.wait_ge(T.sem.s3, 1)
+
+
+def _give_S(g, T, topo, b, dst_core, eng):
+    lo, hi = W * b, W * b + W
+    n = _send(g, topo, [(dst_core, _q(T.S_q, lo, hi), _q(T.S_q, lo, hi), eng, T.sem.s_in)], T.sem.sent)
+    n += _send(g, topo, [(dst_core, T.S_s[:, lo:hi], T.S_s[:, lo:hi], eng, T.sem.s_in)], T.sem.sent)
+    return n
+
+
+def _relay(g, core, T, topo, plan):
+    cores = list(T.cores)
+    me = plan["relays"][core]
+    src, dests = me["src"], me["dests"]
+    fan = _fan_engines(topo, core, cores, dests)
+    allof = [e for p in fan for e in p]
+    sent = 0
+    for b, r in me["jobs"]:
+        _make_S(g, T, b)
+        sent += _give_S(g, T, topo, b, cores[r], allof)
+    hop = len(_bits(topo.mask(cores[src], core)))
+    lo, hi = W * src, W * src + W
+    g.wait_ge(T.sem.hq, hop)
+    sent += _send(g, topo, [(cores[t], _q(T.land_q, lo, hi), _q(T.r_q, W * i, W * i + W), fan[i], T.sem["in%d" % src])
+                            for i, t in enumerate(dests)], T.sem.sent)
+    g.wait_ge(T.sem.hs, hop)
+    sent += _send(g, topo, [(cores[t], T.land_s[:, lo:hi], T.r_s[:, W * i:W * i + W], fan[i], T.sem["in%d" % src])
+                            for i, t in enumerate(dests)], T.sem.sent)
+    g.wait_ge(T.sem.sent, sent)
+
+
+def _arrival_count(topo, cores, plan, src, dst):
+    for via, ds in plan["ships"][src]:
+        if dst in ds:
+            if topo.chip(cores[src]) == topo.chip(cores[dst]):
+                return 2 * len(_home_engines(topo, cores[src], cores, plan, src, dst))
+            sender = cores[src] if via is None else via
+            return 2 * len(_fan_engines(topo, sender, cores, ds)[ds.index(dst)])
+    return 0
+
+
+def _rank(g, core, T, topo, plan, rank):
+    cores = list(T.cores)
+    sem = T.sem
+    ships = plan["ships"][rank]
+    order = [t for via, ds in ships for t in ds] + [rank]
+    mates_here = [r for r in plan["members"][topo.chip(core)] if r != rank]
+    V, S, TE = g.vector, g.scalar, g.tensor
+    Relu = ActivationFunctionType.Relu
+
+    g.sync.dma_start(T.a_t[:], T.a[:]).then_inc(sem.la, 16)
+    for k, c in enumerate(order):
+        q = g.scalar if k % 2 == 0 else g.sync
+        q.dma_start(T.b_t[:, E * k:E * k + E], T.b[:, E * c:E * c + E]).then_inc(sem["lb%d" % k], 16)
+
+    sb = plan["makes"][rank]
+    _make_S(g, T, sb)
+    sent = 0
+    for r in mates_here:
+        sent += _give_S(g, T, topo, sb, cores[r], _bits(topo.mask(core, cores[r])))
+
+    def quant_b(k):
+        V.wait_ge(sem["lb%d" % k], 16)
+        V.quantize_mx(T.b_q[:, W * k:W * k + W], T.b_s[:, W * k:W * k + W], T.b_t[:, E * k:E * k + E]).then_inc(sem["qb%d" % k], 1)
+
+    def bank(k, i):
+        c0 = 512 * (2 * (k % 2) + i)
+        return T.z[:, c0:c0 + W]
+
+    def col(k, b):
+        return T.g_t[:, E * k + b:E * k + E:4]
+
+    V.wait_ge(sem.la, 16)
+    V.quantize_mx(T.a_q[:], T.a_s[:], T.a_t[:]).then_inc(sem.qa, 1)
+    quant_b(0)
+    for k in range(NR):
+        V.wait_ge(sem["ma%d" % k], 1)
+        V.tensor_scalar(col(k, 0), bank(k, 0), CF, 0.0, AluOpType.mult, AluOpType.max).then_inc(sem["r0%d" % k], 1)
+        if k + 1 < NR:
+            quant_b(k + 1)
+        V.wait_ge(sem["r0%d" % k], 1)
+        V.wait_ge(sem["as%d" % k], 3)
+        V.quantize_mx(T.g_q[:, W * k:W * k + W], T.g_s[:, W * k:W * k + W], T.g_t[:, E * k:E * k + E]).then_inc(sem["gq%d" % k], 1)
+
+    for k in range(NR):
+        S.wait_ge(sem["mb%d" % k], 1)
+        S.activation(col(k, 2), bank(k, 1), Relu, scale=CF).then_inc(sem["as%d" % k], 1)
+        S.activation(col(k, 3), bank(k, 1), Relu, scale=-CF).then_inc(sem["as%d" % k], 1)
+        S.wait_ge(sem["ma%d" % k], 1)
+        S.wait_ge(sem["r0%d" % k], 1)
+        S.activation(col(k, 1), bank(k, 0), Relu, scale=-CF).then_inc(sem["as%d" % k], 1)
+
+    TE.wait_ge(sem.qa, 1)
+    for k in range(NR):
+        TE.wait_ge(sem["qb%d" % k], 1)
+        if k >= 2:
+            TE.wait_ge(sem["r0%d" % (k - 2)], 1)
+            TE.wait_ge(sem["as%d" % (k - 2)], 3)
+        for i, name in enumerate(("ma", "mb")):
+            TE.matmul_mx(bank(k, i), T.a_q[:, W * i:W * i + W], T.a_s[:, W * i:W * i + W],
+                         T.b_q[:, W * k:W * k + W], T.b_s[:, W * k:W * k + W], True, True).then_inc(sem["%s%d" % (name, k)], 1)
+
+    k = 0
+    mine = (W * rank, W * rank + W)
+    for via, ds in ships:
+        for j in range(len(ds)):
+            g.wait_ge(sem["gq%d" % (k + j)], 1)
+        lo, hi = W * k, W * (k + len(ds))
+        if via is not None:
+            eng = _bits(topo.mask(core, via))
+            sent += _send(g, topo, [(via, _q(T.r_q, 0, hi - lo), _q(T.g_q, lo, hi), eng, sem.hq)], sem.sent)
+            sent += _send(g, topo, [(via, T.r_s[:, 0:hi - lo], T.g_s[:, lo:hi], eng, sem.hs)], sem.sent)
+        else:
+            if topo.chip(cores[ds[0]]) == topo.chip(core):
+                fan = [_home_engines(topo, core, cores, plan, rank, ds[0])]
+            else:
+                fan = _fan_engines(topo, core, cores, ds)
+            sent += _send(g, topo, [(cores[t], _q(T.land_q, mine[0], mine[1]), _q(T.g_q, lo + W * j, lo + W * j + W),
+                                     fan[j], sem["in%d" % rank]) for j, t in enumerate(ds)], sem.sent)
+            sent += _send(g, topo, [(cores[t], T.land_s[:, mine[0]:mine[1]], T.g_s[:, lo + W * j:lo + W * j + W],
+                                     fan[j], sem["in%d" % rank]) for j, t in enumerate(ds)], sem.sent)
+        k += len(ds)
+
+    s_total = 0
+    for r in mates_here:
+        s_total += 2 * len(_bits(topo.mask(cores[r], core)))
+    for h, info in plan["relays"].items():
+        for b, r in info["jobs"]:
+            if r == rank:
+                s_total += 2 * len(_bits(topo.mask(h, cores[info["dests"][0]])))
+    TE.wait_ge(sem.s3, 1)
+    TE.wait_ge(sem.s_in, s_total)
+    srcs = sorted(range(NR), key=lambda r: (plan["kind"][(r, rank)], r))
+    for n, r in enumerate(srcs):
+        if r == rank:
+            TE.wait_ge(sem["gq%d" % (NR - 1)], 1)
+            cq, cs, lo = T.g_q, T.g_s, W * (NR - 1)
+        else:
+            TE.wait_ge(sem["in%d" % r], _arrival_count(topo, cores, plan, r, rank))
+            cq, cs, lo = T.land_q, T.land_s, W * r
+        for b in range(4):
+            mm = TE.matmul_mx(T.d[:, 512 * b:512 * b + W], T.S_q[:, W * b:W * b + W], T.S_s[:, W * b:W * b + W],
+                              cq[:, lo:lo + W], cs[:, lo:lo + W], n == 0, n == NR - 1)
+            if n == NR - 1:
+                mm.then_inc(sem["dd%d" % b], 1)
+
+    for b in range(4):
+        out, src = T.y_t[:, b:E:4], T.d[:, 512 * b:512 * b + W]
+        if b % 2 == 0:
+            V.wait_ge(sem["dd%d" % b], 1)
+            V.tensor_copy(out, src).then_inc(sem.yc, 1)
+        else:
+            S.wait_ge(sem["dd%d" % b], 1)
+            S.activation(out, src, ActivationFunctionType.Copy).then_inc(sem.yc, 1)
+    g.sync.wait_ge(sem.yc, 4)
+    g.sync.dma_start(T.y[:], T.y_t[:]).then_inc(sem.st, 16)
+    g.sync.wait_ge(sem.st, 16)
+    g.wait_ge(sem.sent, sent)
+
+
+def rank_program(g, core, T, topo):
+    plan = _plan(list(T.cores), topo)
+    rank = T.rank_of(core)
+    if rank is not None:
+        _rank(g, core, T, topo, plan, rank)
+    elif core in plan["relays"]:
+        _relay(g, core, T, topo, plan)

@@ -27,7 +27,7 @@ SCRATCH = {
     "z": ("psum", [128, 4 * 512], "float32"),
     "d": ("psum", [128, 4 * 512], "float32"),
 }
-SEMAPHORES = (["la", "qa", "s1", "s2", "s3", "s_in", "hq", "hs", "sent", "yc", "st"]
+SEMAPHORES = (["la", "qa", "s1", "s2", "s3", "s_in", "hq0", "hq1", "hs0", "hs1", "sent", "yc", "st"]
               + ["%s%d" % (n, k) for n in ("lb", "qb", "ma", "mb", "r0", "as", "gq", "in") for k in range(NR)]
               + ["dd%d" % b for b in range(4)])
 
@@ -57,10 +57,17 @@ def _plan(cores, topo):
     def can(s, o):
         return all(topo.may_write(s, cores[t]) for t in members[o])
 
+    def seq(some, i):
+        out = []
+        for j in range(max([len(members[o]) for o in some] + [0])):
+            for x, o in enumerate(some):
+                out.append((o, members[o][(j + i + x) % len(members[o])]))
+        return out
+
     ships = {r: [] for r in range(n)}
     relays = {}
     makes = {}
-    kind = {}
+    est = {}
     for ch in chips:
         plane = [o for o in chips if o == ch or topo.same_plane(ch, o)]
         near = [o for o in plane if o != ch]
@@ -69,43 +76,49 @@ def _plan(cores, topo):
         far = far[turn:] + far[:turn]
         free = [k for k in every if topo.chip(k) == ch and k not in cores]
         load = {}
-        own_way, handed, via = {}, {}, {}
+        handed, must = {}, {}
         for r in members[ch]:
             s = cores[r]
-            open_ = [o for o in far + near if can(s, o)]
-            own_way[r] = open_[0]
-            handed[r] = [o for o in far + near if o != open_[0]]
-            load[topo.die(s)] = load.get(topo.die(s), 0) + 1
+            handed[r] = [o for o in far + near if not can(s, o)]
+            must[r] = len(handed[r]) > 0
+            if not must[r]:
+                handed[r] = list(near)
+            load[topo.die(s)] = load.get(topo.die(s), 0) + sum(len(members[o]) for o in far + near if o not in handed[r])
         mine = []
-        for some in (far, near):
-            for r in members[ch]:
-                for o in handed[r]:
-                    if o in some:
-                        h = min([k for k in free if k not in mine and can(k, o)],
-                                key=lambda k: (load.get(topo.die(k), 0), k))
-                        mine.append(h)
-                        load[topo.die(h)] = load.get(topo.die(h), 0) + 1
-                        via[(r, o)] = h
-                        relays[h] = {"src": r, "dests": members[o], "jobs": []}
-        for r in members[ch]:
-            for i, o in enumerate(handed[r]):
-                ships[r].append((via[(r, o)], members[o]))
-                for t in members[o]:
-                    kind[(r, t)] = 3 + i
-            ships[r].append((None, members[own_way[r]]))
-            for t in members[own_way[r]]:
-                kind[(r, t)] = 2
+        for i, r in enumerate(members[ch]):
+            via = {}
+            for o in handed[r]:
+                h = min([k for k in free if k not in mine and can(k, o)],
+                        key=lambda k: (load.get(topo.die(k), 0), k))
+                mine.append(h)
+                load[topo.die(h)] = load.get(topo.die(h), 0) + len(members[o])
+                via[o] = h
+                relays[h] = {"src": r, "dests": [], "S": None, "to": []}
+            two = seq(handed[r], i)
+            one = seq([o for o in far + near if o not in handed[r]], i)
+            for o, t in (two + one if must[r] else one[:1] + two + one[1:]):
+                k = len(ships[r])
+                if o in via:
+                    ships[r].append((via[o], len(relays[via[o]]["dests"]), t))
+                    relays[via[o]]["dests"].append(t)
+                    est[(r, t)] = k + 10
+                else:
+                    ships[r].append((None, 0, t))
+                    est[(r, t)] = k + 5
             for t in members[ch]:
                 if t != r:
-                    ships[r].append((None, [t]))
-                    kind[(r, t)] = 1
-            kind[(r, r)] = 0
-        for i, r in enumerate(members[ch]):
+                    est[(r, t)] = len(ships[r]) + 4
+                    ships[r].append((None, 0, t))
+            est[(r, r)] = len(ships[r]) + 0.5
             makes[r] = i
-        rest = [(b, r) for b in range(len(members[ch]), 4) for r in members[ch]]
-        for i, job in enumerate(rest):
-            relays[mine[i % len(mine)]]["jobs"].append(job)
-    return {"members": members, "ships": ships, "relays": relays, "makes": makes, "kind": kind}
+        groups = [[b, list(members[ch])] for b in range(len(members[ch]), 4)]
+        while len(groups) < len(mine) and len(groups[-1][1]) > 1:
+            b, to = groups.pop()
+            groups += [[b, [t]] for t in to]
+        for j, (b, to) in enumerate(groups):
+            relays[mine[j]]["S"] = b
+            relays[mine[j]]["to"] = to
+    return {"members": members, "ships": ships, "relays": relays, "makes": makes, "est": est}
 
 
 def _send(g, topo, items, local_sem):
@@ -127,13 +140,9 @@ def _q(buf, lo, hi):
     return buf[:, lo:hi].bitcast(dt.uint8)
 
 
-def _fan_engines(topo, src_core, cores, dests):
-    return _parts(_bits(topo.mask(src_core, cores[dests[0]])), len(dests))
-
-
 def _home_engines(topo, core, cores, plan, rank, dst):
     on = _bits(topo.mask(core, cores[dst]))
-    away = [t for via, ds in plan["ships"][rank] if via is None for t in ds if topo.chip(cores[t]) != topo.chip(core)]
+    away = [t for via, slot, t in plan["ships"][rank] if via is None and topo.chip(cores[t]) != topo.chip(core)]
     off = _bits(topo.mask(core, cores[away[0]])) if away else []
     left = [e for e in on if e not in off]
     return left if left else on
@@ -149,41 +158,50 @@ def _make_S(g, T, b):
     g.wait_ge(T.sem.s3, 1)
 
 
-def _give_S(g, T, topo, b, dst_core, eng):
+def _give_S(g, T, topo, b, dst_cores, fan):
     lo, hi = W * b, W * b + W
-    n = _send(g, topo, [(dst_core, _q(T.S_q, lo, hi), _q(T.S_q, lo, hi), eng, T.sem.s_in)], T.sem.sent)
-    n += _send(g, topo, [(dst_core, T.S_s[:, lo:hi], T.S_s[:, lo:hi], eng, T.sem.s_in)], T.sem.sent)
+    n = _send(g, topo, [(c, _q(T.S_q, lo, hi), _q(T.S_q, lo, hi), fan[i], T.sem.s_in)
+                        for i, c in enumerate(dst_cores)], T.sem.sent)
+    n += _send(g, topo, [(c, T.S_s[:, lo:hi], T.S_s[:, lo:hi], fan[i], T.sem.s_in)
+                         for i, c in enumerate(dst_cores)], T.sem.sent)
     return n
+
+
+def _relay_fan(topo, core, cores, plan):
+    me = plan["relays"][core]
+    eng = _bits(topo.mask(core, cores[me["dests"][0]]))
+    return me["to"], _parts(eng, len(me["to"]))
 
 
 def _relay(g, core, T, topo, plan):
     cores = list(T.cores)
     me = plan["relays"][core]
     src, dests = me["src"], me["dests"]
-    fan = _fan_engines(topo, core, cores, dests)
-    allof = [e for p in fan for e in p]
     sent = 0
-    for b, r in me["jobs"]:
-        _make_S(g, T, b)
-        sent += _give_S(g, T, topo, b, cores[r], allof)
+    if me["S"] is not None:
+        to, fan = _relay_fan(topo, core, cores, plan)
+        _make_S(g, T, me["S"])
+        sent += _give_S(g, T, topo, me["S"], [cores[r] for r in to], fan)
     hop = len(_bits(topo.mask(cores[src], core)))
     lo, hi = W * src, W * src + W
-    g.wait_ge(T.sem.hq, hop)
-    sent += _send(g, topo, [(cores[t], _q(T.land_q, lo, hi), _q(T.r_q, W * i, W * i + W), fan[i], T.sem["in%d" % src])
-                            for i, t in enumerate(dests)], T.sem.sent)
-    g.wait_ge(T.sem.hs, hop)
-    sent += _send(g, topo, [(cores[t], T.land_s[:, lo:hi], T.r_s[:, W * i:W * i + W], fan[i], T.sem["in%d" % src])
-                            for i, t in enumerate(dests)], T.sem.sent)
+    for i, t in enumerate(dests):
+        eng = _bits(topo.mask(core, cores[t]))
+        g.wait_ge(T.sem["hq%d" % i], hop)
+        sent += _send(g, topo, [(cores[t], _q(T.land_q, lo, hi), _q(T.r_q, W * i, W * i + W), eng, T.sem["in%d" % src])],
+                      T.sem.sent)
+        g.wait_ge(T.sem["hs%d" % i], hop)
+        sent += _send(g, topo, [(cores[t], T.land_s[:, lo:hi], T.r_s[:, W * i:W * i + W], eng, T.sem["in%d" % src])],
+                      T.sem.sent)
     g.wait_ge(T.sem.sent, sent)
 
 
 def _arrival_count(topo, cores, plan, src, dst):
-    for via, ds in plan["ships"][src]:
-        if dst in ds:
+    for via, slot, t in plan["ships"][src]:
+        if t == dst:
             if topo.chip(cores[src]) == topo.chip(cores[dst]):
                 return 2 * len(_home_engines(topo, cores[src], cores, plan, src, dst))
             sender = cores[src] if via is None else via
-            return 2 * len(_fan_engines(topo, sender, cores, ds)[ds.index(dst)])
+            return 2 * len(_bits(topo.mask(sender, cores[dst])))
     return 0
 
 
@@ -191,7 +209,7 @@ def _rank(g, core, T, topo, plan, rank):
     cores = list(T.cores)
     sem = T.sem
     ships = plan["ships"][rank]
-    order = [t for via, ds in ships for t in ds] + [rank]
+    order = [t for via, slot, t in ships] + [rank]
     mates_here = [r for r in plan["members"][topo.chip(core)] if r != rank]
     V, S, TE = g.vector, g.scalar, g.tensor
     Relu = ActivationFunctionType.Relu
@@ -205,7 +223,7 @@ def _rank(g, core, T, topo, plan, rank):
     _make_S(g, T, sb)
     sent = 0
     for r in mates_here:
-        sent += _give_S(g, T, topo, sb, cores[r], _bits(topo.mask(core, cores[r])))
+        sent += _give_S(g, T, topo, sb, [cores[r]], [_bits(topo.mask(core, cores[r]))])
 
     def quant_b(k):
         V.wait_ge(sem["lb%d" % k], 16)
@@ -248,37 +266,36 @@ def _rank(g, core, T, topo, plan, rank):
             TE.matmul_mx(bank(k, i), T.a_q[:, W * i:W * i + W], T.a_s[:, W * i:W * i + W],
                          T.b_q[:, W * k:W * k + W], T.b_s[:, W * k:W * k + W], True, True).then_inc(sem["%s%d" % (name, k)], 1)
 
-    k = 0
     mine = (W * rank, W * rank + W)
-    for via, ds in ships:
-        for j in range(len(ds)):
-            g.wait_ge(sem["gq%d" % (k + j)], 1)
-        lo, hi = W * k, W * (k + len(ds))
+    for k, (via, slot, t) in enumerate(ships):
+        g.wait_ge(sem["gq%d" % k], 1)
+        lo, hi = W * k, W * k + W
         if via is not None:
             eng = _bits(topo.mask(core, via))
-            sent += _send(g, topo, [(via, _q(T.r_q, 0, hi - lo), _q(T.g_q, lo, hi), eng, sem.hq)], sem.sent)
-            sent += _send(g, topo, [(via, T.r_s[:, 0:hi - lo], T.g_s[:, lo:hi], eng, sem.hs)], sem.sent)
+            sent += _send(g, topo, [(via, _q(T.r_q, W * slot, W * slot + W), _q(T.g_q, lo, hi), eng, sem["hq%d" % slot])],
+                          sem.sent)
+            sent += _send(g, topo, [(via, T.r_s[:, W * slot:W * slot + W], T.g_s[:, lo:hi], eng, sem["hs%d" % slot])],
+                          sem.sent)
         else:
-            if topo.chip(cores[ds[0]]) == topo.chip(core):
-                fan = [_home_engines(topo, core, cores, plan, rank, ds[0])]
+            if topo.chip(cores[t]) == topo.chip(core):
+                eng = _home_engines(topo, core, cores, plan, rank, t)
             else:
-                fan = _fan_engines(topo, core, cores, ds)
-            sent += _send(g, topo, [(cores[t], _q(T.land_q, mine[0], mine[1]), _q(T.g_q, lo + W * j, lo + W * j + W),
-                                     fan[j], sem["in%d" % rank]) for j, t in enumerate(ds)], sem.sent)
-            sent += _send(g, topo, [(cores[t], T.land_s[:, mine[0]:mine[1]], T.g_s[:, lo + W * j:lo + W * j + W],
-                                     fan[j], sem["in%d" % rank]) for j, t in enumerate(ds)], sem.sent)
-        k += len(ds)
+                eng = _bits(topo.mask(core, cores[t]))
+            sent += _send(g, topo, [(cores[t], _q(T.land_q, mine[0], mine[1]), _q(T.g_q, lo, hi), eng, sem["in%d" % rank])],
+                          sem.sent)
+            sent += _send(g, topo, [(cores[t], T.land_s[:, mine[0]:mine[1]], T.g_s[:, lo:hi], eng, sem["in%d" % rank])],
+                          sem.sent)
 
     s_total = 0
     for r in mates_here:
         s_total += 2 * len(_bits(topo.mask(cores[r], core)))
     for h, info in plan["relays"].items():
-        for b, r in info["jobs"]:
-            if r == rank:
-                s_total += 2 * len(_bits(topo.mask(h, cores[info["dests"][0]])))
+        if info["S"] is not None and rank in info["to"]:
+            to, fan = _relay_fan(topo, h, cores, plan)
+            s_total += 2 * len(fan[to.index(rank)])
     TE.wait_ge(sem.s3, 1)
     TE.wait_ge(sem.s_in, s_total)
-    srcs = sorted(range(NR), key=lambda r: (plan["kind"][(r, rank)], r))
+    srcs = sorted(range(NR), key=lambda r: (plan["est"][(r, rank)], r))
     for n, r in enumerate(srcs):
         if r == rank:
             TE.wait_ge(sem["gq%d" % (NR - 1)], 1)

from concourse.bass import DstId, RemoteDMATransfer
from concourse.mybir import dt, AluOpType, ActivationFunctionType

NR = 8
W = 128
E = 4 * W
CF = 0.043

SCRATCH = {
    "a_t": ("sbuf", [128, 2 * E], "bfloat16"),
    "b_t": ("sbuf", [128, NR * E], "bfloat16"),
    "g_t": ("sbuf", [128, NR * E], "bfloat16"),
    "S_t": ("sbuf", [128, 4 * E], "bfloat16"),
    "a_q": ("sbuf", [128, 2 * W], "float8_e4m3fn_x4"),
    "a_s": ("sbuf", [128, 2 * W], "uint8"),
    "b_q": ("sbuf", [128, NR * W], "float8_e4m3fn_x4"),
    "b_s": ("sbuf", [128, NR * W], "uint8"),
    "g_q": ("sbuf", [128, NR * W], "float8_e4m3fn_x4"),
    "g_s": ("sbuf", [128, NR * W], "uint8"),
    "land_q": ("sbuf", [128, NR * W], "float8_e4m3fn_x4"),
    "land_s": ("sbuf", [128, NR * W], "uint8"),
    "S_q": ("sbuf", [128, 4 * W], "float8_e4m3fn_x4"),
    "S_s": ("sbuf", [128, 4 * W], "uint8"),
    "r_q": ("sbuf", [128, 2 * W], "float8_e4m3fn_x4"),
    "r_s": ("sbuf", [128, 2 * W], "uint8"),
    "y_t": ("sbuf", [128, E], "float32"),
    "z": ("psum", [128, 4 * 512], "float32"),
    "d": ("psum", [128, 4 * 512], "float32"),
}
SEMAPHORES = (["la", "qa", "s1", "s2", "s3", "s_in", "hq0", "hq1", "hs0", "hs1", "sent", "yc", "st"]
              + ["%s%d" % (n, k) for n in ("lb", "qb", "ma", "mb", "r0", "as", "gq", "in") for k in range(NR)]
              + ["dd%d" % b for b in range(4)])


def _bits(m):
    return [i for i in range(m.bit_length()) if (m >> i) & 1]


def _mask(engines):
    return sum(1 << i for i in engines)


def _parts(engines, k):
    n = len(engines) // k
    return [engines[i * n:(i + 1) * n] for i in range(k)]


def _plan(cores, topo):
    n = len(cores)
    every = range(topo.CHIPS * topo.CORES_PER_CHIP)
    chips = []
    for c in cores:
        if topo.chip(c) not in chips:
            chips.append(topo.chip(c))
    members = {ch: [r for r in range(n) if topo.chip(cores[r]) == ch] for ch in chips}

    def can(s, o):
        return all(topo.may_write(s, cores[t]) for t in members[o])

    def seq(some, i):
        out = []
        for j in range(max([len(members[o]) for o in some] + [0])):
            for x, o in enumerate(some):
                out.append((o, members[o][(j + i + x) % len(members[o])]))
        return out

    ships = {r: [] for r in range(n)}
    relays = {}
    makes = {}
    est = {}
    for ch in chips:
        plane = [o for o in chips if o == ch or topo.same_plane(ch, o)]
        near = [o for o in plane if o != ch]
        far = [o for o in chips if o not in plane]
        turn = plane.index(ch) % max(len(far), 1)
        far = far[turn:] + far[:turn]
        free = [k for k in every if topo.chip(k) == ch and k not in cores]
        load = {}
        handed, must = {}, {}
        for r in members[ch]:
            s = cores[r]
            handed[r] = [o for o in far + near if not can(s, o)]
            must[r] = len(handed[r]) > 0
            if not must[r]:
                handed[r] = list(near)
            load[topo.die(s)] = load.get(topo.die(s), 0) + sum(len(members[o]) for o in far + near if o not in handed[r])
        mine = []
        for i, r in enumerate(members[ch]):
            via = {}
            for o in handed[r]:
                h = min([k for k in free if k not in mine and can(k, o)],
                        key=lambda k: (load.get(topo.die(k), 0), k))
                mine.append(h)
                load[topo.die(h)] = load.get(topo.die(h), 0) + len(members[o])
                via[o] = h
                relays[h] = {"src": r, "dests": [], "S": None, "to": []}
            two = seq(handed[r], i)
            one = seq([o for o in far + near if o not in handed[r]], i)
            for o, t in (two + one if must[r] else one[:1] + two + one[1:]):
                k = len(ships[r])
                if o in via:
                    ships[r].append((via[o], len(relays[via[o]]["dests"]), t))
                    relays[via[o]]["dests"].append(t)
                    est[(r, t)] = k + 10
                else:
                    ships[r].append((None, 0, t))
                    est[(r, t)] = k + 5
            for t in members[ch]:
                if t != r:
                    est[(r, t)] = len(ships[r]) + 4
                    ships[r].append((None, 0, t))
            est[(r, r)] = len(ships[r]) + 0.5
            makes[r] = i
        groups = [[b, list(members[ch])] for b in range(len(members[ch]), 4)]
        while len(groups) < len(mine) and len(groups[-1][1]) > 1:
            b, to = groups.pop()
            groups += [[b, [t]] for t in to]
        for j, (b, to) in enumerate(groups):
            relays[mine[j]]["S"] = b
            relays[mine[j]]["to"] = to
    return {"members": members, "ships": ships, "relays": relays, "makes": makes, "est": est}


def _send(g, topo, items, local_sem):
    if len(items) == 1:
        dst, out, src, eng, rsem = items[0]
        rid, pid, se = topo.addr(dst)
        g.remote_dma(out, src, rsem, local_sem, pid, rid, _mask(eng))
    else:
        trs = []
        for dst, out, src, eng, rsem in items:
            rid, pid, se = topo.addr(dst)
            trs.append(RemoteDMATransfer(dst_ids=[DstId(rid=rid, pnc=pid)], dma_engine_mask=_mask(eng),
                                         remote_sem=rsem, src=src, dst=out))
        g.remote_dma_fused(trs, local_sem=local_sem)
    return sum(len(it[3]) for it in items)


def _q(buf, lo, hi):
    return buf[:, lo:hi].bitcast(dt.uint8)


def _home_engines(topo, core, cores, plan, rank, dst):
    on = _bits(topo.mask(core, cores[dst]))
    away = [t for via, slot, t in plan["ships"][rank] if via is None and topo.chip(cores[t]) != topo.chip(core)]
    off = _bits(topo.mask(core, cores[away[0]])) if away else []
    left = [e for e in on if e not in off]
    return left if left else on


def _make_S(g, T, b):
    t = T.S_t[:, E * b:E * b + E]
    g.vector.memset(t, 1.0).then_inc(T.sem.s1, 1)
    g.wait_ge(T.sem.s1, 1)
    g.affine_select(t, t, [[-1, E]], AluOpType.is_equal, 0.0, b, 4).then_inc(T.sem.s2, 1)
    g.vector.wait_ge(T.sem.s2, 1)
    g.vector.quantize_mx(T.S_q[:, W * b:W * b + W], T.S_s[:, W * b:W * b + W], t).then_inc(T.sem.s3, 1)
    g.wait_ge(T.sem.s3, 1)


def _give_S(g, T, topo, b, dst_cores, fan):
    lo, hi = W * b, W * b + W
    n = _send(g, topo, [(c, _q(T.S_q, lo, hi), _q(T.S_q, lo, hi), fan[i], T.sem.s_in)
                        for i, c in enumerate(dst_cores)], T.sem.sent)
    n += _send(g, topo, [(c, T.S_s[:, lo:hi], T.S_s[:, lo:hi], fan[i], T.sem.s_in)
                         for i, c in enumerate(dst_cores)], T.sem.sent)
    return n


def _relay_fan(topo, core, cores, plan):
    me = plan["relays"][core]
    eng = _bits(topo.mask(core, cores[me["dests"][0]]))
    return me["to"], _parts(eng, len(me["to"]))


def _relay(g, core, T, topo, plan):
    cores = list(T.cores)
    me = plan["relays"][core]
    src, dests = me["src"], me["dests"]
    sent = 0
    if me["S"] is not None:
        to, fan = _relay_fan(topo, core, cores, plan)
        _make_S(g, T, me["S"])
        sent += _give_S(g, T, topo, me["S"], [cores[r] for r in to], fan)
    hop = len(_bits(topo.mask(cores[src], core)))
    lo, hi = W * src, W * src + W
    for i, t in enumerate(dests):
        eng = _bits(topo.mask(core, cores[t]))
        g.wait_ge(T.sem["hq%d" % i], hop)
        sent += _send(g, topo, [(cores[t], _q(T.land_q, lo, hi), _q(T.r_q, W * i, W * i + W), eng, T.sem["in%d" % src])],
                      T.sem.sent)
        g.wait_ge(T.sem["hs%d" % i], hop)
        sent += _send(g, topo, [(cores[t], T.land_s[:, lo:hi], T.r_s[:, W * i:W * i + W], eng, T.sem["in%d" % src])],
                      T.sem.sent)
    g.wait_ge(T.sem.sent, sent)


def _arrival_count(topo, cores, plan, src, dst):
    for via, slot, t in plan["ships"][src]:
        if t == dst:
            if topo.chip(cores[src]) == topo.chip(cores[dst]):
                return 2 * len(_home_engines(topo, cores[src], cores, plan, src, dst))
            sender = cores[src] if via is None else via
            return 2 * len(_bits(topo.mask(sender, cores[dst])))
    return 0


def _rank(g, core, T, topo, plan, rank):
    cores = list(T.cores)
    sem = T.sem
    ships = plan["ships"][rank]
    order = [t for via, slot, t in ships] + [rank]
    mates_here = [r for r in plan["members"][topo.chip(core)] if r != rank]
    V, S, TE = g.vector, g.scalar, g.tensor
    Relu = ActivationFunctionType.Relu

    g.sync.dma_start(T.a_t[:], T.a[:]).then_inc(sem.la, 16)
    for k, c in enumerate(order):
        q = g.scalar if k % 2 == 0 else g.sync
        q.dma_start(T.b_t[:, E * k:E * k + E], T.b[:, E * c:E * c + E]).then_inc(sem["lb%d" % k], 16)

    sb = plan["makes"][rank]
    _make_S(g, T, sb)
    sent = 0
    for r in mates_here:
        sent += _give_S(g, T, topo, sb, [cores[r]], [_bits(topo.mask(core, cores[r]))])

    def quant_b(k):
        V.wait_ge(sem["lb%d" % k], 16)
        V.quantize_mx(T.b_q[:, W * k:W * k + W], T.b_s[:, W * k:W * k + W], T.b_t[:, E * k:E * k + E]).then_inc(sem["qb%d" % k], 1)

    def bank(k, i):
        c0 = 512 * (2 * (k % 2) + i)
        return T.z[:, c0:c0 + W]

    def col(k, b):
        return T.g_t[:, E * k + b:E * k + E:4]

    V.wait_ge(sem.la, 16)
    V.quantize_mx(T.a_q[:], T.a_s[:], T.a_t[:]).then_inc(sem.qa, 1)
    quant_b(0)
    for k in range(NR):
        V.wait_ge(sem["ma%d" % k], 1)
        V.tensor_scalar(col(k, 0), bank(k, 0), CF, 0.0, AluOpType.mult, AluOpType.max).then_inc(sem["r0%d" % k], 1)
        if k + 1 < NR:
            quant_b(k + 1)
        V.wait_ge(sem["r0%d" % k], 1)
        V.wait_ge(sem["as%d" % k], 3)
        V.quantize_mx(T.g_q[:, W * k:W * k + W], T.g_s[:, W * k:W * k + W], T.g_t[:, E * k:E * k + E]).then_inc(sem["gq%d" % k], 1)

    for k in range(NR):
        S.wait_ge(sem["mb%d" % k], 1)
        S.activation(col(k, 2), bank(k, 1), Relu, scale=CF).then_inc(sem["as%d" % k], 1)
        S.activation(col(k, 3), bank(k, 1), Relu, scale=-CF).then_inc(sem["as%d" % k], 1)
        S.wait_ge(sem["ma%d" % k], 1)
        S.wait_ge(sem["r0%d" % k], 1)
        S.activation(col(k, 1), bank(k, 0), Relu, scale=-CF).then_inc(sem["as%d" % k], 1)

    TE.wait_ge(sem.qa, 1)
    for k in range(NR):
        TE.wait_ge(sem["qb%d" % k], 1)
        if k >= 2:
            TE.wait_ge(sem["r0%d" % (k - 2)], 1)
            TE.wait_ge(sem["as%d" % (k - 2)], 3)
        for i, name in enumerate(("ma", "mb")):
            TE.matmul_mx(bank(k, i), T.a_q[:, W * i:W * i + W], T.a_s[:, W * i:W * i + W],
                         T.b_q[:, W * k:W * k + W], T.b_s[:, W * k:W * k + W], True, True).then_inc(sem["%s%d" % (name, k)], 1)

    mine = (W * rank, W * rank + W)
    for k, (via, slot, t) in enumerate(ships):
        g.wait_ge(sem["gq%d" % k], 1)
        lo, hi = W * k, W * k + W
        if via is not None:
            eng = _bits(topo.mask(core, via))
            sent += _send(g, topo, [(via, _q(T.r_q, W * slot, W * slot + W), _q(T.g_q, lo, hi), eng, sem["hq%d" % slot])],
                          sem.sent)
            sent += _send(g, topo, [(via, T.r_s[:, W * slot:W * slot + W], T.g_s[:, lo:hi], eng, sem["hs%d" % slot])],
                          sem.sent)
        else:
            if topo.chip(cores[t]) == topo.chip(core):
                eng = _home_engines(topo, core, cores, plan, rank, t)
            else:
                eng = _bits(topo.mask(core, cores[t]))
            sent += _send(g, topo, [(cores[t], _q(T.land_q, mine[0], mine[1]), _q(T.g_q, lo, hi), eng, sem["in%d" % rank])],
                          sem.sent)
            sent += _send(g, topo, [(cores[t], T.land_s[:, mine[0]:mine[1]], T.g_s[:, lo:hi], eng, sem["in%d" % rank])],
                          sem.sent)

    s_total = 0
    for r in mates_here:
        s_total += 2 * len(_bits(topo.mask(cores[r], core)))
    for h, info in plan["relays"].items():
        if info["S"] is not None and rank in info["to"]:
            to, fan = _relay_fan(topo, h, cores, plan)
            s_total += 2 * len(fan[to.index(rank)])
    TE.wait_ge(sem.s3, 1)
    TE.wait_ge(sem.s_in, s_total)
    srcs = sorted(range(NR), key=lambda r: (plan["est"][(r, rank)], r))
    for n, r in enumerate(srcs):
        if r == rank:
            TE.wait_ge(sem["gq%d" % (NR - 1)], 1)
            cq, cs, lo = T.g_q, T.g_s, W * (NR - 1)
        else:
            TE.wait_ge(sem["in%d" % r], _arrival_count(topo, cores, plan, r, rank))
            cq, cs, lo = T.land_q, T.land_s, W * r
        for b in range(4):
            mm = TE.matmul_mx(T.d[:, 512 * b:512 * b + W], T.S_q[:, W * b:W * b + W], T.S_s[:, W * b:W * b + W],
                              cq[:, lo:lo + W], cs[:, lo:lo + W], n == 0, n == NR - 1)
            if n == NR - 1:
                mm.then_inc(sem["dd%d" % b], 1)

    for b in range(4):
        out, src = T.y_t[:, b:E:4], T.d[:, 512 * b:512 * b + W]
        if b % 2 == 0:
            V.wait_ge(sem["dd%d" % b], 1)
            V.tensor_copy(out, src).then_inc(sem.yc, 1)
        else:
            S.wait_ge(sem["dd%d" % b], 1)
            S.activation(out, src, ActivationFunctionType.Copy).then_inc(sem.yc, 1)
    g.sync.wait_ge(sem.yc, 4)
    g.sync.dma_start(T.y[:], T.y_t[:]).then_inc(sem.st, 16)
    g.sync.wait_ge(sem.st, 16)
    g.wait_ge(sem.sent, sent)


def rank_program(g, core, T, topo):
    plan = _plan(list(T.cores), topo)
    rank = T.rank_of(core)
    if rank is not None:
        _rank(g, core, T, topo, plan, rank)
    elif core in plan["relays"]:
        _relay(g, core, T, topo, plan)
